import numpy as np
CORES = [1,129,9,137,17,145,25,153,33,161,41,169,49,177,57,185,65,193,73,201,81,209,89,217,97,225,105,233,113,241,121,249]
N = 32
def setup_inputs(rng):
    return {"x": rng.standard_normal((N, 128, 256), dtype=np.float32)}
def reference(x):
    s = x.sum(axis=0, dtype=np.float64).astype(x.dtype)
    b = 256 // N
    return {"y": np.stack([s[:, r * b:(r + 1) * b] for r in range(N)])}

from concourse.bass import DstId, RemoteDMATransfer

SCRATCH = {
    "xs": ("sbuf", [128, 256], "float32"),
    "lane": ("sbuf", [128, 64], "float32"),
    "mate": ("sbuf", [128, 32], "float32"),
    "part": ("dram", [16, 128, 8], "float32"),
    "tot": ("dram", [128, 8], "float32"),
}
SEMAPHORES = ["loaded", "got", "mated", "parts", "fin", "sent", "stored"]

RANK_CORE = 1
COLLECTOR = 0
LANE_CORES = ((2, 3, 6, 7), (6, 7, 2, 3))


def rank_program(g, core, T, topo):
    h, k, j = topo.host(core), topo.chip(core), core % 8
    base = core - j
    p = k % 2
    lanes = LANE_CORES[h]
    sem = T.sem

    def to(dst):
        rid, pid = topo.addr(dst, core)
        return DstId(rid=rid, pnc=pid)

    if j == RANK_CORE:
        g.sync.dma_start(T.xs[:], T.x[:]).then_inc(sem.loaded, 16)
        g.wait_ge(sem.loaded, 16)
        g.remote_dma_fused(
            [RemoteDMATransfer(dst_ids=[to(base + c)], dma_engine_mask=0xF << (4 * l), remote_sem=sem.got,
                               src=T.xs[:, 64 * l:64 * l + 64], dst=T.lane[:])
             for l, c in enumerate(lanes)],
            local_sem=sem.sent)
        g.sync.wait_ge(sem.fin, 16)
        g.sync.dma_start(T.y[:], T.tot[:]).then_inc(sem.stored, 16)
        g.wait_ge(sem.sent, 16)
        g.wait_ge(sem.stored, 16)

    elif j in lanes:
        l = lanes.index(j)
        g.wait_ge(sem.got, 4)
        peer = core + 8 if p == 0 else core - 8
        g.remote_dma_fused(
            [RemoteDMATransfer(dst_ids=[to(peer)], dma_engine_mask=0xF << (4 * i), remote_sem=sem.mated,
                               src=T.lane[:, 16 * q:16 * q + 16], dst=T.mate[:, 16 * i:16 * i + 16])
             for i, q in enumerate((1 - p, 3 - p))],
            local_sem=sem.sent)
        g.wait_ge(sem.mated, 8)
        slot = 8 * h + k // 2
        sends = []
        for i in range(2):
            q = p + 2 * i
            for hd in range(2):
                dst = 128 * hd + 8 * (4 * l + q) + COLLECTOR
                sends.append(RemoteDMATransfer(
                    dst_ids=[to(dst)], dma_engine_mask=0x3 << (2 * (2 * i + hd)), remote_sem=sem.parts, alu_op=1,
                    srcs=[T.lane[:, 16 * q + 8 * hd:16 * q + 8 * hd + 8], T.mate[:, 16 * i + 8 * hd:16 * i + 8 * hd + 8]],
                    dsts=[T.part[slot]]))
        g.remote_dma_fused(sends, local_sem=sem.sent)
        g.wait_ge(sem.sent, 16)

    elif j == COLLECTOR:
        g.wait_ge(sem.parts, 32)
        g.remote_dma_fused(
            [RemoteDMATransfer(dst_ids=[to(base + RANK_CORE)], dma_engine_mask=0xFFFF, remote_sem=sem.fin, alu_op=1,
                               srcs=[T.part[i] for i in range(16)], dsts=[T.tot[:]])],
            local_sem=sem.sent)
        g.wait_ge(sem.sent, 16)
